import numpy as np
import ml_dtypes


def mxq(x, axis, fmt="e4m3"):
    dtype, down = {"e4m3": (ml_dtypes.float8_e4m3fn, 7), "e5m2": (ml_dtypes.float8_e5m2, 14)}[fmt]
    v = np.moveaxis(np.asarray(x, np.float32).astype(ml_dtypes.bfloat16).astype(np.float64), axis, -1)
    blocks = v.reshape(v.shape[:-1] + (-1, 32))
    amax = np.abs(blocks).max(-1, keepdims=True)
    byte = np.maximum(np.where(amax > 0, np.frexp(amax)[1] - 1 + 127, 0) - down, 1)
    scale = np.exp2(byte - 127.0)
    codes = (blocks / scale).astype(np.float32).astype(dtype).astype(np.float64)
    return np.moveaxis((codes * scale).reshape(v.shape), -1, axis)


WIDE = False


def mx_kscale(k):
    if not WIDE:
        return np.ones(k)
    levels = np.array([10, -10, 5, -5, 0])
    if k % 512:
        return np.exp2(np.random.permutation(np.resize(levels, k // 32))).repeat(32)
    a = np.empty((k // 512, 16))
    for p in range(k // 512):
        a[p, :8] = np.random.permutation(np.resize(levels, 8))
        for g in range(8):
            far = levels[np.abs(levels - a[p, g]) >= 10]
            a[p, g + 8] = far[np.random.randint(len(far))]
    return np.exp2(a.ravel()).repeat(32)


def f64(x):
    return np.asarray(x).astype(np.float64)


def striped(idx):
    return np.tile(idx.reshape(-1, 16).T, (8, 1)).astype(np.uint16)


def unstriped(offs):
    return offs[:16].T.reshape(-1).astype(np.int64)


def pack_weight(w):
    k, n = w.shape
    w = f64(np.asarray(w, np.float32).astype(ml_dtypes.bfloat16)).reshape(k // 32, 32, n)
    amax = np.abs(w).max(1)
    byte = np.clip(np.where(amax > 0, np.frexp(amax)[1] - 1 + 127 - 7, 1), 1, 254)
    scaled = (w * np.exp2(127.0 - byte)[:, None, :]).reshape(k, n).astype(np.float32)
    words = np.ascontiguousarray(scaled.reshape(k // 512, 128, 4, n).transpose(0, 1, 3, 2)).astype(ml_dtypes.float8_e4m3fn).view(np.uint8)
    return words, np.ascontiguousarray(byte.astype(np.uint8).reshape(k // 512, 16, n))


def unpack_weight(words, scales):
    g, p, n, _ = words.shape
    vals = np.ascontiguousarray(words).view(ml_dtypes.float8_e4m3fn).astype(np.float64) * np.repeat(np.exp2(scales.astype(np.float64) - 127.0), 8, axis=1)[..., None]
    return vals.transpose(0, 1, 3, 2).reshape(g * 512, n)


def relu(v):
    return np.maximum(v, 0.0)


K, T, S, V = 512, 1024, 512, 512
P = 2 ** 7


def setup_inputs():
    n = np.random.standard_normal
    s = mx_kscale(K)[:, None]
    packed_xT = pack_weight(n((K, T)) * s)
    packed_eT = pack_weight(n((K, T)) * s)
    return {
        "x_words": packed_xT[0],
        "x_scales": packed_xT[1],
        "e_words": packed_eT[0],
        "e_scales": packed_eT[1],
        "hx": (n((K, V)) / np.sqrt(K) / s).astype(np.float32),
        "hs": (n((K, V)) / np.sqrt(K) / s).astype(np.float32),
        "qn": (np.tile(np.random.uniform(0.5, 1.5, T), (P, 1))).astype(np.float32),
        "own": (np.random.uniform(0.5, 1.5, (V, 1))).astype(np.float32),
        "offs": striped(np.random.permutation(T)[:S]),
    }


def reference(x_words, x_scales, e_words, e_scales, hx, hs, qn, own, offs):
    hxq = mxq(f64(hx), 0, "e4m3")
    xq = unpack_weight(x_words, x_scales)[:, unstriped(offs)]
    y = hxq.T @ xq
    dd = relu(f64(qn)[:1][:, unstriped(offs)] - y + f64(own))
    kk = np.exp(-0.5 * dd)
    hsq = mxq(f64(hs), 0, "e4m3")
    e_offs = unpack_weight(e_words, e_scales)[:, unstriped(offs)]
    z = hsq.T @ e_offs
    cr = hsq.T @ xq + hxq.T @ e_offs
    return np.tanh(kk * (z - cr - dd))

@@ -1,0 +1,191 @@
+from contextlib import ExitStack
+
+import concourse.mybir as mybir
+
+F32 = mybir.dt.float32
+BF16 = mybir.dt.bfloat16
+I32 = mybir.dt.int32
+U32 = mybir.dt.uint32
+U16 = mybir.dt.uint16
+U8 = mybir.dt.uint8
+FP8X4 = mybir.dt.float8_e4m3fn_x4
+ALU = mybir.AluOpType
+ACT = mybir.ActivationFunctionType
+
+P = 128
+PACK = 4
+K = 512
+T = 1024
+S = 512
+V = 512
+HALF = V // 2
+TILES = V // P
+
+FLOPS = 4 * 2 * K * V * S
+
+
+def tile_picked_yksd_tanh_p_kernel(
+    tc, x_words, x_scales, e_words, e_scales, hx, hs, qn, own, offs, out
+):
+    nc = tc.nc
+    with ExitStack() as ctx:
+        keep = ctx.enter_context(tc.tile_pool(name="keep", bufs=1))
+        psum = ctx.enter_context(tc.psum_pool(name="psum", bufs=1))
+
+        offsets = keep.tile([P, S // 16], U16, name="offsets")
+        nc.sync.dma_start(offsets[:], offs)
+
+        def load_scales(name, dram):
+            table = keep.tile([P, T], U8, name=name, align_bytes=64)
+            rows = dram[0].bitcast(I32)
+            for quad in range(4):
+                nc.sync.dma_start(
+                    table[:].bitcast(I32)[32 * quad:32 * quad + 32, :],
+                    rows[4 * quad:4 * quad + 4, :].partition_broadcast(8),
+                )
+            return table
+
+        def load_words(name, dram, queue):
+            table = keep.tile([P, T], I32, name=name, align_bytes=64)
+            queue.dma_start(table[:], dram[0].rearrange("p c r -> p (c r)").bitcast(I32))
+            return table
+
+        def load_half(name, dram, h):
+            raw = keep.tile([P, PACK, HALF], F32, name=name)
+            nc.sync.dma_start(raw[:], dram.rearrange("(p j) t -> p j t", j=PACK)[:, :, h * HALF:(h + 1) * HALF])
+            return raw
+
+        def gather(name, table, dtype):
+            picked = keep.tile([P, S], dtype, name=name, align_bytes=64)
+            nc.vector.tensor_copy(picked[:], table.indirect(offsets[:]))
+            return picked
+
+        def interleave(name, raw):
+            grouped = keep.tile([P, HALF, PACK], BF16, name=name, align_bytes=64)
+            nc.scalar.activation(
+                grouped[:].rearrange("p (c i) j -> p c j i", i=4),
+                raw[:].rearrange("p j (c i) -> p c j i", i=4),
+                ACT.Copy,
+            )
+            return grouped
+
+        def quantize(name, grouped):
+            codes = keep.tile([P, HALF], U32, name=name + "_codes", align_bytes=64)
+            scales = keep.tile([P, HALF], U8, name=name + "_scales", align_bytes=64)
+            nc.vector.quantize_mx(codes[:].bitcast(FP8X4), scales[:], grouped[:].rearrange("p t j -> p (t j)"))
+            return codes, scales
+
+        def negate(name, grouped):
+            minus = keep.tile([P, HALF, PACK], BF16, name=name, align_bytes=64)
+            nc.vector.tensor_scalar(
+                minus[:].rearrange("p t j -> p (t j)"), grouped[:].rearrange("p t j -> p (t j)"), -1.0, None, ALU.mult
+            )
+            return minus
+
+        def product(bank, stationary, cols, moving, start, stop):
+            nc.tensor.matmul_mx(
+                out=bank[:],
+                lhsT=stationary[0][:, cols].bitcast(FP8X4),
+                lhsT_scale=stationary[1][:, cols],
+                rhs=moving[0][:].bitcast(FP8X4),
+                rhs_scale=moving[1][:],
+                start=start,
+                stop=stop,
+            )
+
+        def interleave_negated(name, raw):
+            grouped = keep.tile([P, HALF, PACK], BF16, name=name, align_bytes=64)
+            nc.scalar.activation(
+                grouped[:].rearrange("p (c i) j -> p c j i", i=4),
+                raw[:].rearrange("p j (c i) -> p c j i", i=4),
+                ACT.Copy,
+                scale=-1.0,
+            )
+            return grouped
+
+        def cols_of(i):
+            return slice((i % 2) * P, (i % 2 + 1) * P)
+
+        xs_table = load_scales("xs_table", x_scales)
+        xw_table = load_words("xw_table", x_words, nc.scalar)
+        hx_raw = [load_half("hx_raw0", hx, 0)]
+        qn_table = keep.tile([P, T], F32, name="qn_table")
+        nc.sync.dma_start(qn_table[:], qn)
+        es_table = load_scales("es_table", e_scales)
+        hx_raw.append(load_half("hx_raw1", hx, 1))
+        hs_raw = [load_half("hs_raw0", hs, 0)]
+        ew_table = load_words("ew_table", e_words, nc.sync)
+        hs_raw.append(load_half("hs_raw1", hs, 1))
+        own_cols = keep.tile([P, TILES], F32, name="own_cols")
+        with nc.allow_non_contiguous_dma(reason="one value a partition and output tile"):
+            nc.gpsimd.dma_start(own_cols[:], own.rearrange("(i p) o -> p (i o)", p=P))
+
+        warm = keep.tile([P, 1], F32, name="warm")
+        nc.vector.memset(warm[:], 0.0)
+        warm_out = keep.tile([P, 1], F32, name="warm_out")
+        nc.scalar.activation(warm_out[:], warm[:], ACT.Exp)
+
+        nhx, phs, nhs, hs_bf, arg, kk, nu = {}, {}, {}, {}, {}, {}, {}
+
+        def distance(i):
+            ny = psum.tile([P, S], F32, name="ny%d" % i)
+            product(ny, nhx[i // 2], cols_of(i), x, True, True)
+            arg[i] = keep.tile([P, S], F32, name="arg%d" % i)
+            nc.vector.scalar_tensor_tensor(arg[i][:], ny[:], own_cols[:, i:i + 1], q[:], ALU.add, ALU.add)
+
+        def kernel_value(i):
+            dd = keep.tile([P, S], F32, name="dd%d" % i)
+            nc.scalar.activation(dd[:], arg[i][:], ACT.Relu)
+            kk[i] = keep.tile([P, S], F32, name="kk%d" % i)
+            nc.scalar.activation(kk[i][:], dd[:], ACT.Exp, scale=-0.5)
+
+        def quantize_hs(h):
+            minus = negate("nhs_bf%d" % h, hs_bf[h])
+            phs[h] = quantize("phs%d" % h, hs_bf[h])
+            nhs[h] = quantize("nhs%d" % h, minus)
+
+        def scores(i):
+            w = psum.tile([P, S], F32, name="w%d" % i)
+            product(w, nhx[i // 2], cols_of(i), e, True, False)
+            product(w, phs[i // 2], cols_of(i), e, False, False)
+            product(w, nhs[i // 2], cols_of(i), x, False, True)
+            nu[i] = keep.tile([P, S], F32, name="nu%d" % i)
+            nc.vector.scalar_tensor_tensor(nu[i][:], arg[i][:], 0.0, w[:], ALU.max, ALU.subtract)
+
+        def finish(i):
+            prod = keep.tile([P, S], F32, name="prod%d" % i)
+            nc.vector.tensor_tensor(prod[:], nu[i][:], kk[i][:], ALU.mult)
+            res = keep.tile([P, S], F32, name="res%d" % i)
+            nc.scalar.activation(res[:], prod[:], ACT.Tanh, scale=-1.0)
+            nc.sync.dma_start(out[i * P:(i + 1) * P, :], res[:])
+
+        xs = gather("xs", xs_table[:], U8)
+        xw = gather("xw", xw_table[:].bitcast(U32), U32)
+        x = (xw, xs)
+        es = gather("es", es_table[:], U8)
+        nhx[0] = quantize("nhx0", interleave_negated("nhx_bf0", hx_raw[0]))
+        q = gather("q", qn_table[:], F32)
+        nhx_bf1 = interleave_negated("nhx_bf1", hx_raw[1])
+        distance(0)
+        distance(1)
+        hs_bf[0] = interleave("hs_bf0", hs_raw[0])
+        nhx[1] = quantize("nhx1", nhx_bf1)
+        ew = gather("ew", ew_table[:].bitcast(U32), U32)
+        e = (ew, es)
+        kernel_value(0)
+        quantize_hs(0)
+        hs_bf[1] = interleave("hs_bf1", hs_raw[1])
+        distance(2)
+        distance(3)
+        kernel_value(1)
+        scores(0)
+        scores(1)
+        quantize_hs(1)
+        kernel_value(2)
+        kernel_value(3)
+        finish(0)
+        finish(1)
+        scores(2)
+        scores(3)
+        finish(2)
+        finish(3)

@@ -1,6 +1,7 @@
 from contextlib import ExitStack
 
 import concourse.mybir as mybir
+from concourse.masks import make_identity
 
 F32 = mybir.dt.float32
 BF16 = mybir.dt.bfloat16
@@ -20,6 +21,8 @@ S = 512
 V = 512
 HALF = V // 2
 TILES = V // P
+BANK = 512
+PER_PART = T // P
 
 FLOPS = 4 * 2 * K * V * S
 
@@ -30,162 +33,168 @@ def tile_picked_yksd_tanh_p_kernel(
     nc = tc.nc
     with ExitStack() as ctx:
         keep = ctx.enter_context(tc.tile_pool(name="keep", bufs=1))
+        shared = ctx.enter_context(tc.tile_pool(name="shared", bufs=1))
         psum = ctx.enter_context(tc.psum_pool(name="psum", bufs=1))
+
+        def sbuf(name, shape, dtype, after=None):
+            return keep.tile(shape, dtype, name=name, tag=after or name, align_bytes=64)
 
         offsets = keep.tile([P, S // 16], U16, name="offsets")
         nc.sync.dma_start(offsets[:], offs)
 
-        def load_scales(name, dram):
-            table = keep.tile([P, T], U8, name=name, align_bytes=64)
+        def load_scales(name, dram, queues):
+            table = sbuf(name, [P, T], U8)
             rows = dram[0].bitcast(I32)
             for quad in range(4):
-                nc.sync.dma_start(
+                queues[quad].dma_start(
                     table[:].bitcast(I32)[32 * quad:32 * quad + 32, :],
                     rows[4 * quad:4 * quad + 4, :].partition_broadcast(8),
                 )
             return table
 
-        def load_words(name, dram, queue):
-            table = keep.tile([P, T], I32, name=name, align_bytes=64)
-            queue.dma_start(table[:], dram[0].rearrange("p c r -> p (c r)").bitcast(I32))
+        def load_words(name, dram):
+            table = sbuf(name, [P, T], I32)
+            nc.sync.dma_start(table[:], dram[0].rearrange("p c r -> p (c r)").bitcast(I32))
             return table
 
-        def load_half(name, dram, h):
-            raw = keep.tile([P, PACK, HALF], F32, name=name)
-            nc.sync.dma_start(raw[:], dram.rearrange("(p j) t -> p j t", j=PACK)[:, :, h * HALF:(h + 1) * HALF])
+        def load_columns(name, dram, first, count):
+            raw = sbuf(name, [P, PACK, count], F32)
+            nc.sync.dma_start(raw[:], dram.rearrange("(p j) t -> p j t", j=PACK)[:, :, first:first + count])
             return raw
 
-        def gather(name, table, dtype):
-            picked = keep.tile([P, S], dtype, name=name, align_bytes=64)
+        def gather(name, table, dtype, offset):
+            if offset is None:
+                picked = sbuf(name, [P, S], dtype)
+            else:
+                picked = shared.tile([P, S], dtype, name=name, offset=offset, align_bytes=64)
             nc.vector.tensor_copy(picked[:], table.indirect(offsets[:]))
             return picked
 
-        def interleave(name, raw):
-            grouped = keep.tile([P, HALF, PACK], BF16, name=name, align_bytes=64)
+        def interleave(name, raw, sign):
+            grouped = sbuf(name, [P, HALF * PACK], BF16)
             nc.scalar.activation(
-                grouped[:].rearrange("p (c i) j -> p c j i", i=4),
-                raw[:].rearrange("p j (c i) -> p c j i", i=4),
+                grouped[:].rearrange("p (c i j) -> p c j i", i=4, j=PACK),
+                raw.rearrange("p j (c i) -> p c j i", i=4),
                 ACT.Copy,
+                scale=sign,
             )
             return grouped
 
-        def quantize(name, grouped):
-            codes = keep.tile([P, HALF], U32, name=name + "_codes", align_bytes=64)
-            scales = keep.tile([P, HALF], U8, name=name + "_scales", align_bytes=64)
-            nc.vector.quantize_mx(codes[:].bitcast(FP8X4), scales[:], grouped[:].rearrange("p t j -> p (t j)"))
+        def quantize(name, grouped, after=None):
+            codes = sbuf(name + "_codes", [P, HALF], U32, after)
+            scales = sbuf(name + "_scales", [P, HALF], U8)
+            nc.vector.quantize_mx(codes[:].bitcast(FP8X4), scales[:], grouped[:])
             return codes, scales
 
-        def negate(name, grouped):
-            minus = keep.tile([P, HALF, PACK], BF16, name=name, align_bytes=64)
-            nc.vector.tensor_scalar(
-                minus[:].rearrange("p t j -> p (t j)"), grouped[:].rearrange("p t j -> p (t j)"), -1.0, None, ALU.mult
-            )
-            return minus
-
-        def product(bank, stationary, cols, moving, start, stop):
+        def product(bank, stationary, i, moving, start, stop):
+            codes, scales = stationary[i // 2]
+            cols = slice((i % 2) * P, (i % 2 + 1) * P)
             nc.tensor.matmul_mx(
                 out=bank[:],
-                lhsT=stationary[0][:, cols].bitcast(FP8X4),
-                lhsT_scale=stationary[1][:, cols],
+                lhsT=codes[:, cols].bitcast(FP8X4),
+                lhsT_scale=scales[:, cols],
                 rhs=moving[0][:].bitcast(FP8X4),
                 rhs_scale=moving[1][:],
                 start=start,
                 stop=stop,
             )
 
-        def interleave_negated(name, raw):
-            grouped = keep.tile([P, HALF, PACK], BF16, name=name, align_bytes=64)
-            nc.scalar.activation(
-                grouped[:].rearrange("p (c i) j -> p c j i", i=4),
-                raw[:].rearrange("p j (c i) -> p c j i", i=4),
-                ACT.Copy,
-                scale=-1.0,
+        qn_cols = sbuf("qn_cols", [P, PER_PART], F32)
+        nc.sync.dma_start(qn_cols[:], qn[0].rearrange("(p c) -> p c", c=PER_PART))
+        xs_table = load_scales("xs_table", x_scales, [nc.sync] * 4)
+        xw_table = load_words("xw_table", x_words)
+        hx_raw = load_columns("hx_raw", hx, 0, V)
+        es_table = load_scales("es_table", e_scales, [nc.sync] * 4)
+        ew_table = load_words("ew_table", e_words)
+        hs_raw = [load_columns("hs_raw%d" % h, hs, h * HALF, HALF) for h in range(2)]
+
+        identity = sbuf("identity", [P, P], F32)
+        make_identity(nc, identity[:])
+        own_rows = sbuf("own_rows", [P, P], F32)
+        nc.gpsimd.memset(own_rows[:], 0.0)
+        nc.gpsimd.dma_start(own_rows[0:TILES, :], own.rearrange("(i p) o -> i (p o)", p=P))
+
+        warm = sbuf("warm", [P, 1], F32)
+        nc.scalar.activation(warm[:], identity[:, 0:1], ACT.Exp)
+
+        qn_table = shared.tile([P, T], F32, name="qn_table", offset=0, align_bytes=64)
+        for b in range(T // BANK):
+            spread = psum.tile([P, BANK // P, P], F32, name="spread%d" % b, tag="w%d" % (2 + b))
+            for c in range(BANK // P):
+                col = b * (BANK // P) + c
+                nc.tensor.transpose(spread[:, c, :], qn_cols[:, col:col + 1].to_broadcast([P, P]), identity[:])
+            nc.scalar.copy(
+                qn_table[:].rearrange("r (p b c) -> r b p c", b=T // BANK, c=BANK // P)[:, b],
+                spread[:].rearrange("r c p -> r p c"),
             )
-            return grouped
+        own_turned = psum.tile([P, P], F32, name="own_turned", tag="w1")
+        nc.tensor.transpose(own_turned[:], own_rows[:], identity[:])
+        own_cols = sbuf("own_cols", [P, TILES], F32)
+        nc.scalar.copy(own_cols[:], own_turned[:, 0:TILES])
 
-        def cols_of(i):
-            return slice((i % 2) * P, (i % 2 + 1) * P)
+        nhx, phs, nhs = {}, {}, {}
+        xs = gather("xs", xs_table[:], U8, None)
+        xw = gather("xw", xw_table[:].bitcast(U32), U32, None)
+        x = (xw, xs)
+        q = gather("q", qn_table[:], F32, None)
+        es = gather("es", es_table[:], U8, 0)
+        nhx_bf = [interleave("nhx_bf%d" % h, hx_raw[:, :, h * HALF:(h + 1) * HALF], -1.0) for h in range(2)]
+        hs_bf = [interleave("hs_bf%d" % h, hs_raw[h][:], 1.0) for h in range(2)]
+        nhx[0] = quantize("nhx0", nhx_bf[0])
+        ew = gather("ew", ew_table[:].bitcast(U32), U32, 2048)
+        e = (ew, es)
+        nhx[1] = quantize("nhx1", nhx_bf[1])
 
-        xs_table = load_scales("xs_table", x_scales)
-        xw_table = load_words("xw_table", x_words, nc.scalar)
-        hx_raw = [load_half("hx_raw0", hx, 0)]
-        qn_table = keep.tile([P, T], F32, name="qn_table")
-        nc.sync.dma_start(qn_table[:], qn)
-        es_table = load_scales("es_table", e_scales)
-        hx_raw.append(load_half("hx_raw1", hx, 1))
-        hs_raw = [load_half("hs_raw0", hs, 0)]
-        ew_table = load_words("ew_table", e_words, nc.sync)
-        hs_raw.append(load_half("hs_raw1", hs, 1))
-        own_cols = keep.tile([P, TILES], F32, name="own_cols")
-        with nc.allow_non_contiguous_dma(reason="one value a partition and output tile"):
-            nc.gpsimd.dma_start(own_cols[:], own.rearrange("(i p) o -> p (i o)", p=P))
+        arg, kk, nu = {}, {}, {}
+        last = TILES - 1
 
-        warm = keep.tile([P, 1], F32, name="warm")
-        nc.vector.memset(warm[:], 0.0)
-        warm_out = keep.tile([P, 1], F32, name="warm_out")
-        nc.scalar.activation(warm_out[:], warm[:], ACT.Exp)
-
-        nhx, phs, nhs, hs_bf, arg, kk, nu = {}, {}, {}, {}, {}, {}, {}
-
-        def distance(i):
+        def distance(i, after=None):
             ny = psum.tile([P, S], F32, name="ny%d" % i)
-            product(ny, nhx[i // 2], cols_of(i), x, True, True)
-            arg[i] = keep.tile([P, S], F32, name="arg%d" % i)
+            product(ny, nhx, i, x, True, True)
+            arg[i] = sbuf("arg%d" % i, [P, S], F32, after)
             nc.vector.scalar_tensor_tensor(arg[i][:], ny[:], own_cols[:, i:i + 1], q[:], ALU.add, ALU.add)
 
-        def kernel_value(i):
-            dd = keep.tile([P, S], F32, name="dd%d" % i)
-            nc.scalar.activation(dd[:], arg[i][:], ACT.Relu)
-            kk[i] = keep.tile([P, S], F32, name="kk%d" % i)
-            nc.scalar.activation(kk[i][:], dd[:], ACT.Exp, scale=-0.5)
+        for i in range(TILES):
+            distance(i)
 
-        def quantize_hs(h):
-            minus = negate("nhs_bf%d" % h, hs_bf[h])
+        banks = []
+        for i in range(TILES):
+            banks.append(psum.tile([P, S], F32, name="w%d" % i, tag="w%d" % i))
+            product(banks[i], nhx, i, e, True, False)
+
+        for h in range(2):
+            minus = sbuf("nhs_bf%d" % h, [P, HALF * PACK], BF16)
+            nc.vector.tensor_scalar(minus[:], hs_bf[h][:], -1.0, None, ALU.mult)
             phs[h] = quantize("phs%d" % h, hs_bf[h])
             nhs[h] = quantize("nhs%d" % h, minus)
 
+        dd = sbuf("dd", [P, TILES, S], F32, "hs_raw1")
+
+        def kernel_value(i):
+            nc.scalar.activation(dd[:, i, :], arg[i][:], ACT.Relu)
+            kk[i] = sbuf("kk%d" % i, [P, S], F32)
+            nc.scalar.activation(kk[i][:], dd[:, i, :], ACT.Exp, scale=-0.5)
+
         def scores(i):
-            w = psum.tile([P, S], F32, name="w%d" % i)
-            product(w, nhx[i // 2], cols_of(i), e, True, False)
-            product(w, phs[i // 2], cols_of(i), e, False, False)
-            product(w, nhs[i // 2], cols_of(i), x, False, True)
-            nu[i] = keep.tile([P, S], F32, name="nu%d" % i)
-            nc.vector.scalar_tensor_tensor(nu[i][:], arg[i][:], 0.0, w[:], ALU.max, ALU.subtract)
+            product(banks[i], phs, i, e, False, False)
+            product(banks[i], nhs, i, x, False, True)
+            nu[i] = sbuf("nu%d" % i, [P, S], F32)
+            nc.vector.scalar_tensor_tensor(nu[i][:], arg[i][:], 0.0, banks[i][:], ALU.max, ALU.subtract)
 
-        def finish(i):
-            prod = keep.tile([P, S], F32, name="prod%d" % i)
-            nc.vector.tensor_tensor(prod[:], nu[i][:], kk[i][:], ALU.mult)
-            res = keep.tile([P, S], F32, name="res%d" % i)
+        def finish(engine, i, first, count, after=None):
+            cols = slice(first, first + count)
+            prod = sbuf("prod%d_%d" % (i, first), [P, count], F32, after)
+            engine.tensor_tensor(prod[:], nu[i][:, cols], kk[i][:, cols], ALU.mult)
+            res = sbuf("res%d_%d" % (i, first), [P, count], F32)
             nc.scalar.activation(res[:], prod[:], ACT.Tanh, scale=-1.0)
-            nc.sync.dma_start(out[i * P:(i + 1) * P, :], res[:])
+            nc.sync.dma_start(out[i * P:(i + 1) * P, cols], res[:])
 
-        xs = gather("xs", xs_table[:], U8)
-        xw = gather("xw", xw_table[:].bitcast(U32), U32)
-        x = (xw, xs)
-        es = gather("es", es_table[:], U8)
-        nhx[0] = quantize("nhx0", interleave_negated("nhx_bf0", hx_raw[0]))
-        q = gather("q", qn_table[:], F32)
-        nhx_bf1 = interleave_negated("nhx_bf1", hx_raw[1])
-        distance(0)
-        distance(1)
-        hs_bf[0] = interleave("hs_bf0", hs_raw[0])
-        nhx[1] = quantize("nhx1", nhx_bf1)
-        ew = gather("ew", ew_table[:].bitcast(U32), U32)
-        e = (ew, es)
-        kernel_value(0)
-        quantize_hs(0)
-        hs_bf[1] = interleave("hs_bf1", hs_raw[1])
-        distance(2)
-        distance(3)
-        kernel_value(1)
-        scores(0)
-        scores(1)
-        quantize_hs(1)
-        kernel_value(2)
-        kernel_value(3)
-        finish(0)
-        finish(1)
-        scores(2)
-        scores(3)
-        finish(2)
-        finish(3)
+        for i in range(TILES):
+            kernel_value(i)
+        for i in range(TILES):
+            scores(i)
+        finish(nc.gpsimd, 0, 0, S, "nhs_bf1")
+        finish(nc.vector, 1, 0, S, "arg2")
+        finish(nc.vector, 2, 0, S)
+        finish(nc.vector, last, 0, S // 2)
+        finish(nc.vector, last, S // 2, S // 2)

@@ -23,6 +23,9 @@ HALF = V // 2
 TILES = V // P
 BANK = 512
 PER_PART = T // P
+QUADRANT = 32
+HALF_TABLE_BYTES = T * 4 // 2
+LINE = 4
 
 FLOPS = 4 * 2 * K * V * S
 
@@ -42,13 +45,13 @@ def tile_picked_yksd_tanh_p_kernel(
         offsets = keep.tile([P, S // 16], U16, name="offsets")
         nc.sync.dma_start(offsets[:], offs)
 
-        def load_scales(name, dram, queues):
+        def load_scales(name, dram):
             table = sbuf(name, [P, T], U8)
             rows = dram[0].bitcast(I32)
-            for quad in range(4):
-                queues[quad].dma_start(
-                    table[:].bitcast(I32)[32 * quad:32 * quad + 32, :],
-                    rows[4 * quad:4 * quad + 4, :].partition_broadcast(8),
+            for quad in range(P // QUADRANT):
+                nc.sync.dma_start(
+                    table[:].bitcast(I32)[QUADRANT * quad:QUADRANT * (quad + 1), :],
+                    rows[4 * quad:4 * quad + 4, :].partition_broadcast(QUADRANT // 4),
                 )
             return table
 
@@ -62,7 +65,7 @@ def tile_picked_yksd_tanh_p_kernel(
             nc.sync.dma_start(raw[:], dram.rearrange("(p j) t -> p j t", j=PACK)[:, :, first:first + count])
             return raw
 
-        def gather(name, table, dtype, offset):
+        def gather(name, table, dtype, offset=None):
             if offset is None:
                 picked = sbuf(name, [P, S], dtype)
             else:
@@ -73,49 +76,47 @@ def tile_picked_yksd_tanh_p_kernel(
         def interleave(name, raw, sign):
             grouped = sbuf(name, [P, HALF * PACK], BF16)
             nc.scalar.activation(
-                grouped[:].rearrange("p (c i j) -> p c j i", i=4, j=PACK),
-                raw.rearrange("p j (c i) -> p c j i", i=4),
+                grouped[:].rearrange("p (c i j) -> p c j i", i=LINE, j=PACK),
+                raw.rearrange("p j (c i) -> p c j i", i=LINE),
                 ACT.Copy,
                 scale=sign,
             )
             return grouped
 
-        def quantize(name, grouped, after=None):
-            codes = sbuf(name + "_codes", [P, HALF], U32, after)
+        def quantize(name, grouped):
+            codes = sbuf(name + "_codes", [P, HALF], U32)
             scales = sbuf(name + "_scales", [P, HALF], U8)
             nc.vector.quantize_mx(codes[:].bitcast(FP8X4), scales[:], grouped[:])
             return codes, scales
 
-        def product(bank, stationary, i, moving, start, stop):
-            codes, scales = stationary[i // 2]
+        def product(bank, halves, i, picked, start, stop):
+            codes, scales = halves[i // 2]
             cols = slice((i % 2) * P, (i % 2 + 1) * P)
             nc.tensor.matmul_mx(
                 out=bank[:],
                 lhsT=codes[:, cols].bitcast(FP8X4),
                 lhsT_scale=scales[:, cols],
-                rhs=moving[0][:].bitcast(FP8X4),
-                rhs_scale=moving[1][:],
+                rhs=picked[0][:].bitcast(FP8X4),
+                rhs_scale=picked[1][:],
                 start=start,
                 stop=stop,
             )
 
         qn_cols = sbuf("qn_cols", [P, PER_PART], F32)
         nc.sync.dma_start(qn_cols[:], qn[0].rearrange("(p c) -> p c", c=PER_PART))
-        xs_table = load_scales("xs_table", x_scales, [nc.sync] * 4)
+        xs_table = load_scales("xs_table", x_scales)
         xw_table = load_words("xw_table", x_words)
         hx_raw = load_columns("hx_raw", hx, 0, V)
-        es_table = load_scales("es_table", e_scales, [nc.sync] * 4)
+        es_table = load_scales("es_table", e_scales)
         ew_table = load_words("ew_table", e_words)
         hs_raw = [load_columns("hs_raw%d" % h, hs, h * HALF, HALF) for h in range(2)]
 
         identity = sbuf("identity", [P, P], F32)
         make_identity(nc, identity[:])
         own_rows = sbuf("own_rows", [P, P], F32)
-        nc.gpsimd.memset(own_rows[:], 0.0)
+        nc.gpsimd.memset(own_rows[0:P // 2, :], 0.0)
         nc.gpsimd.dma_start(own_rows[0:TILES, :], own.rearrange("(i p) o -> i (p o)", p=P))
-
-        warm = sbuf("warm", [P, 1], F32)
-        nc.scalar.activation(warm[:], identity[:, 0:1], ACT.Exp)
+        nc.scalar.activation(own_rows[P // 2:P, :], identity[P // 2:P, :], ACT.Copy, scale=0.0)
 
         qn_table = shared.tile([P, T], F32, name="qn_table", offset=0, align_bytes=64)
         for b in range(T // BANK):
@@ -133,29 +134,26 @@ def tile_picked_yksd_tanh_p_kernel(
         nc.scalar.copy(own_cols[:], own_turned[:, 0:TILES])
 
         nhx, phs, nhs = {}, {}, {}
-        xs = gather("xs", xs_table[:], U8, None)
-        xw = gather("xw", xw_table[:].bitcast(U32), U32, None)
+        xs = gather("xs", xs_table[:], U8)
+        xw = gather("xw", xw_table[:].bitcast(U32), U32)
         x = (xw, xs)
-        q = gather("q", qn_table[:], F32, None)
+        q = gather("q", qn_table[:], F32)
         es = gather("es", es_table[:], U8, 0)
         nhx_bf = [interleave("nhx_bf%d" % h, hx_raw[:, :, h * HALF:(h + 1) * HALF], -1.0) for h in range(2)]
         hs_bf = [interleave("hs_bf%d" % h, hs_raw[h][:], 1.0) for h in range(2)]
         nhx[0] = quantize("nhx0", nhx_bf[0])
-        ew = gather("ew", ew_table[:].bitcast(U32), U32, 2048)
+        ew = gather("ew", ew_table[:].bitcast(U32), U32, HALF_TABLE_BYTES)
         e = (ew, es)
         nhx[1] = quantize("nhx1", nhx_bf[1])
 
         arg, kk, nu = {}, {}, {}
         last = TILES - 1
 
-        def distance(i, after=None):
+        for i in range(TILES):
             ny = psum.tile([P, S], F32, name="ny%d" % i)
             product(ny, nhx, i, x, True, True)
-            arg[i] = sbuf("arg%d" % i, [P, S], F32, after)
+            arg[i] = sbuf("arg%d" % i, [P, S], F32)
             nc.vector.scalar_tensor_tensor(arg[i][:], ny[:], own_cols[:, i:i + 1], q[:], ALU.add, ALU.add)
-
-        for i in range(TILES):
-            distance(i)
 
         banks = []
         for i in range(TILES):
@@ -169,13 +167,12 @@ def tile_picked_yksd_tanh_p_kernel(
             nhs[h] = quantize("nhs%d" % h, minus)
 
         dd = sbuf("dd", [P, TILES, S], F32, "hs_raw1")
-
-        def kernel_value(i):
+        for i in range(TILES):
             nc.scalar.activation(dd[:, i, :], arg[i][:], ACT.Relu)
             kk[i] = sbuf("kk%d" % i, [P, S], F32)
             nc.scalar.activation(kk[i][:], dd[:, i, :], ACT.Exp, scale=-0.5)
 
-        def scores(i):
+        for i in range(TILES):
             product(banks[i], phs, i, e, False, False)
             product(banks[i], nhs, i, x, False, True)
             nu[i] = sbuf("nu%d" % i, [P, S], F32)
@@ -189,10 +186,6 @@ def tile_picked_yksd_tanh_p_kernel(
             nc.scalar.activation(res[:], prod[:], ACT.Tanh, scale=-1.0)
             nc.sync.dma_start(out[i * P:(i + 1) * P, cols], res[:])
 
-        for i in range(TILES):
-            kernel_value(i)
-        for i in range(TILES):
-            scores(i)
         finish(nc.gpsimd, 0, 0, S, "nhs_bf1")
         finish(nc.vector, 1, 0, S, "arg2")
         finish(nc.vector, 2, 0, S)

from contextlib import ExitStack

import concourse.mybir as mybir
from concourse.masks import make_identity

F32 = mybir.dt.float32
BF16 = mybir.dt.bfloat16
I32 = mybir.dt.int32
U32 = mybir.dt.uint32
U16 = mybir.dt.uint16
U8 = mybir.dt.uint8
FP8X4 = mybir.dt.float8_e4m3fn_x4
ALU = mybir.AluOpType
ACT = mybir.ActivationFunctionType

P = 128
PACK = 4
K = 512
T = 1024
S = 512
V = 512
HALF = V // 2
TILES = V // P
BANK = 512
PER_PART = T // P
QUADRANT = 32
HALF_TABLE_BYTES = T * 4 // 2
LINE = 4

FLOPS = 4 * 2 * K * V * S


def tile_picked_yksd_tanh_p_kernel(
    tc, x_words, x_scales, e_words, e_scales, hx, hs, qn, own, offs, out
):
    nc = tc.nc
    with ExitStack() as ctx:
        keep = ctx.enter_context(tc.tile_pool(name="keep", bufs=1))
        shared = ctx.enter_context(tc.tile_pool(name="shared", bufs=1))
        psum = ctx.enter_context(tc.psum_pool(name="psum", bufs=1))

        def sbuf(name, shape, dtype, after=None):
            return keep.tile(shape, dtype, name=name, tag=after or name, align_bytes=64)

        offsets = keep.tile([P, S // 16], U16, name="offsets")
        nc.sync.dma_start(offsets[:], offs)

        def load_scales(name, dram):
            table = sbuf(name, [P, T], U8)
            rows = dram[0].bitcast(I32)
            for quad in range(P // QUADRANT):
                nc.sync.dma_start(
                    table[:].bitcast(I32)[QUADRANT * quad:QUADRANT * (quad + 1), :],
                    rows[4 * quad:4 * quad + 4, :].partition_broadcast(QUADRANT // 4),
                )
            return table

        def load_words(name, dram):
            table = sbuf(name, [P, T], I32)
            nc.sync.dma_start(table[:], dram[0].rearrange("p c r -> p (c r)").bitcast(I32))
            return table

        def load_columns(name, dram, first, count):
            raw = sbuf(name, [P, PACK, count], F32)
            nc.sync.dma_start(raw[:], dram.rearrange("(p j) t -> p j t", j=PACK)[:, :, first:first + count])
            return raw

        def gather(name, table, dtype, offset=None):
            if offset is None:
                picked = sbuf(name, [P, S], dtype)
            else:
                picked = shared.tile([P, S], dtype, name=name, offset=offset, align_bytes=64)
            nc.vector.tensor_copy(picked[:], table.indirect(offsets[:]))
            return picked

        def interleave(name, raw, sign):
            grouped = sbuf(name, [P, HALF * PACK], BF16)
            nc.scalar.activation(
                grouped[:].rearrange("p (c i j) -> p c j i", i=LINE, j=PACK),
                raw.rearrange("p j (c i) -> p c j i", i=LINE),
                ACT.Copy,
                scale=sign,
            )
            return grouped

        def quantize(name, grouped):
            codes = sbuf(name + "_codes", [P, HALF], U32)
            scales = sbuf(name + "_scales", [P, HALF], U8)
            nc.vector.quantize_mx(codes[:].bitcast(FP8X4), scales[:], grouped[:])
            return codes, scales

        def product(bank, halves, i, picked, start, stop):
            codes, scales = halves[i // 2]
            cols = slice((i % 2) * P, (i % 2 + 1) * P)
            nc.tensor.matmul_mx(
                out=bank[:],
                lhsT=codes[:, cols].bitcast(FP8X4),
                lhsT_scale=scales[:, cols],
                rhs=picked[0][:].bitcast(FP8X4),
                rhs_scale=picked[1][:],
                start=start,
                stop=stop,
            )

        qn_cols = sbuf("qn_cols", [P, PER_PART], F32)
        nc.sync.dma_start(qn_cols[:], qn[0].rearrange("(p c) -> p c", c=PER_PART))
        xs_table = load_scales("xs_table", x_scales)
        xw_table = load_words("xw_table", x_words)
        hx_raw = load_columns("hx_raw", hx, 0, V)
        es_table = load_scales("es_table", e_scales)
        ew_table = load_words("ew_table", e_words)
        hs_raw = [load_columns("hs_raw%d" % h, hs, h * HALF, HALF) for h in range(2)]

        identity = sbuf("identity", [P, P], F32)
        make_identity(nc, identity[:])
        own_rows = sbuf("own_rows", [P, P], F32)
        nc.gpsimd.memset(own_rows[0:P // 2, :], 0.0)
        nc.gpsimd.dma_start(own_rows[0:TILES, :], own.rearrange("(i p) o -> i (p o)", p=P))
        nc.scalar.activation(own_rows[P // 2:P, :], identity[P // 2:P, :], ACT.Copy, scale=0.0)

        qn_table = shared.tile([P, T], F32, name="qn_table", offset=0, align_bytes=64)
        for b in range(T // BANK):
            spread = psum.tile([P, BANK // P, P], F32, name="spread%d" % b, tag="w%d" % (2 + b))
            for c in range(BANK // P):
                col = b * (BANK // P) + c
                nc.tensor.transpose(spread[:, c, :], qn_cols[:, col:col + 1].to_broadcast([P, P]), identity[:])
            nc.scalar.copy(
                qn_table[:].rearrange("r (p b c) -> r b p c", b=T // BANK, c=BANK // P)[:, b],
                spread[:].rearrange("r c p -> r p c"),
            )
        own_turned = psum.tile([P, P], F32, name="own_turned", tag="w1")
        nc.tensor.transpose(own_turned[:], own_rows[:], identity[:])
        own_cols = sbuf("own_cols", [P, TILES], F32)
        nc.scalar.copy(own_cols[:], own_turned[:, 0:TILES])

        nhx, phs, nhs = {}, {}, {}
        xs = gather("xs", xs_table[:], U8)
        xw = gather("xw", xw_table[:].bitcast(U32), U32)
        x = (xw, xs)
        q = gather("q", qn_table[:], F32)
        es = gather("es", es_table[:], U8, 0)
        nhx_bf = [interleave("nhx_bf%d" % h, hx_raw[:, :, h * HALF:(h + 1) * HALF], -1.0) for h in range(2)]
        hs_bf = [interleave("hs_bf%d" % h, hs_raw[h][:], 1.0) for h in range(2)]
        nhx[0] = quantize("nhx0", nhx_bf[0])
        ew = gather("ew", ew_table[:].bitcast(U32), U32, HALF_TABLE_BYTES)
        e = (ew, es)
        nhx[1] = quantize("nhx1", nhx_bf[1])

        arg, kk, nu = {}, {}, {}
        last = TILES - 1

        for i in range(TILES):
            ny = psum.tile([P, S], F32, name="ny%d" % i)
            product(ny, nhx, i, x, True, True)
            arg[i] = sbuf("arg%d" % i, [P, S], F32)
            nc.vector.scalar_tensor_tensor(arg[i][:], ny[:], own_cols[:, i:i + 1], q[:], ALU.add, ALU.add)

        banks = []
        for i in range(TILES):
            banks.append(psum.tile([P, S], F32, name="w%d" % i, tag="w%d" % i))
            product(banks[i], nhx, i, e, True, False)

        for h in range(2):
            minus = sbuf("nhs_bf%d" % h, [P, HALF * PACK], BF16)
            nc.vector.tensor_scalar(minus[:], hs_bf[h][:], -1.0, None, ALU.mult)
            phs[h] = quantize("phs%d" % h, hs_bf[h])
            nhs[h] = quantize("nhs%d" % h, minus)

        dd = sbuf("dd", [P, TILES, S], F32, "hs_raw1")
        for i in range(TILES):
            nc.scalar.activation(dd[:, i, :], arg[i][:], ACT.Relu)
            kk[i] = sbuf("kk%d" % i, [P, S], F32)
            nc.scalar.activation(kk[i][:], dd[:, i, :], ACT.Exp, scale=-0.5)

        for i in range(TILES):
            product(banks[i], phs, i, e, False, False)
            product(banks[i], nhs, i, x, False, True)
            nu[i] = sbuf("nu%d" % i, [P, S], F32)
            nc.vector.scalar_tensor_tensor(nu[i][:], arg[i][:], 0.0, banks[i][:], ALU.max, ALU.subtract)

        def finish(engine, i, first, count, after=None):
            cols = slice(first, first + count)
            prod = sbuf("prod%d_%d" % (i, first), [P, count], F32, after)
            engine.tensor_tensor(prod[:], nu[i][:, cols], kk[i][:, cols], ALU.mult)
            res = sbuf("res%d_%d" % (i, first), [P, count], F32)
            nc.scalar.activation(res[:], prod[:], ACT.Tanh, scale=-1.0)
            nc.sync.dma_start(out[i * P:(i + 1) * P, cols], res[:])

        finish(nc.gpsimd, 0, 0, S, "nhs_bf1")
        finish(nc.vector, 1, 0, S, "arg2")
        finish(nc.vector, 2, 0, S)
        finish(nc.vector, last, 0, S // 2)
        finish(nc.vector, last, S // 2, S // 2)
